import numpy as np
import ml_dtypes


def mxq(x, axis, fmt="e4m3"):
    dtype, down = {"e4m3": (ml_dtypes.float8_e4m3fn, 7), "e5m2": (ml_dtypes.float8_e5m2, 14)}[fmt]
    v = np.moveaxis(np.asarray(x, np.float32).astype(ml_dtypes.bfloat16).astype(np.float64), axis, -1)
    blocks = v.reshape(v.shape[:-1] + (-1, 32))
    amax = np.abs(blocks).max(-1, keepdims=True)
    byte = np.maximum(np.where(amax > 0, np.frexp(amax)[1] - 1 + 127, 0) - down, 1)
    scale = np.exp2(byte - 127.0)
    codes = (blocks / scale).astype(np.float32).astype(dtype).astype(np.float64)
    return np.moveaxis((codes * scale).reshape(v.shape), -1, axis)


WIDE = False


def mx_kscale(k):
    if not WIDE:
        return np.ones(k)
    levels = np.array([10, -10, 5, -5, 0])
    if k % 512:
        return np.exp2(np.random.permutation(np.resize(levels, k // 32))).repeat(32)
    a = np.empty((k // 512, 16))
    for p in range(k // 512):
        a[p, :8] = np.random.permutation(np.resize(levels, 8))
        for g in range(8):
            far = levels[np.abs(levels - a[p, g]) >= 10]
            a[p, g + 8] = far[np.random.randint(len(far))]
    return np.exp2(a.ravel()).repeat(32)


def f64(x):
    return np.asarray(x).astype(np.float64)


def striped(idx):
    return np.tile(idx.reshape(-1, 16).T, (8, 1)).astype(np.uint16)


def unstriped(offs):
    return offs[:16].T.reshape(-1).astype(np.int64)


E2M1 = np.array([0.0, 0.5, 1.0, 1.5, 2.0, 3.0, 4.0, 6.0, -0.0, -0.5, -1.0, -1.5, -2.0, -3.0, -4.0, -6.0])


def pack_weight(w, fmt):
    k, n = w.shape
    w = f64(np.asarray(w, np.float32).astype(ml_dtypes.bfloat16)).reshape(k // 32, 32, n)
    amax = np.abs(w).max(1)
    if fmt == "e4m3":
        byte = np.frexp(amax)[1] - 1 + 127 - 7
    else:
        mant, ex = np.frexp(amax / 6.0)
        byte = np.where(mant > 0.5, ex, ex - 1) + 127
    byte = np.clip(np.where(amax > 0, byte, 1), 1, 254)
    scaled = (w * np.exp2(127.0 - byte)[:, None, :]).reshape(k, n).astype(np.float32)
    by_word = np.ascontiguousarray(scaled.reshape(k // 512, 128, 4, n).transpose(0, 1, 3, 2))
    if fmt == "e4m3":
        words = by_word.astype(ml_dtypes.float8_e4m3fn).view(np.uint8)
    else:
        c = by_word.astype(ml_dtypes.float4_e2m1fn).view(np.uint8) & 0xF
        words = (c[..., 0::2] | (c[..., 1::2] << 4)).reshape(k // 512, 128, 2 * n)
    return np.ascontiguousarray(words), np.ascontiguousarray(byte.astype(np.uint8).reshape(k // 512, 16, n))


def unpack_weight(words, scales, fmt):
    g, _, n = scales.shape
    words = np.ascontiguousarray(words).reshape(g, 128, n, -1)
    if fmt == "e4m3":
        vals = words.view(ml_dtypes.float8_e4m3fn).astype(np.float64)
    else:
        nib = np.empty((g, 128, n, 4), np.uint8)
        nib[..., 0::2] = words & 0xF
        nib[..., 1::2] = words >> 4
        vals = E2M1[nib]
    vals = vals * np.repeat(np.exp2(scales.astype(np.float64) - 127.0), 8, axis=1)[..., None]
    return vals.transpose(0, 1, 3, 2).reshape(g * 512, n)


def gelu(v):
    return 0.5 * v * (1.0 + np.tanh(np.sqrt(2.0 / np.pi) * (v + 0.044715 * v**3)))


K, K2, H, T, S = 1536, 512, 1024, 2048, 512


def setup_inputs():
    n = np.random.standard_normal
    s = mx_kscale(K)[:, None]
    s2 = mx_kscale(K2)[:, None]
    u = mx_kscale(H)[:, None]
    d = {}
    d["tab_words"], d["tab_scales"] = pack_weight(n((K, T)) * s, "e4m3")
    d["offs"] = striped(np.random.permutation(T)[:S])
    d["xs_words"], d["xs_scales"] = pack_weight(n((K2, S)) * s2, "e4m3")
    d["w1"] = (n((K, H)) / s / K ** 0.5).astype(np.float32)
    d["w2_words"], d["w2_scales"] = pack_weight(n((K2, H)) / s2 / K2 ** 0.5, "e2m1")
    d["b1"] = (0.5 * n(H)).astype(np.float32)
    d["gain"] = (np.exp(0.3 * n(H)) * u[:, 0]).astype(np.float32)
    d["w3"] = (n((H, H)) / u / H ** 0.5).astype(np.float32)
    d["w4"] = (n((K2, H)) / s2 / K2 ** 0.5).astype(np.float32)
    d["b2"] = (0.6 * n(H)).astype(np.float32)
    return d


def reference(tab_words, tab_scales, offs, xs_words, xs_scales, w1, w2_words, w2_scales, b1, gain, w3, w4, b2):
    v = unpack_weight(tab_words, tab_scales, "e4m3")[:, unstriped(offs)]
    xs = unpack_weight(xs_words, xs_scales, "e4m3")
    w2 = unpack_weight(w2_words, w2_scales, "e2m1")
    a = mxq(f64(w1), 0, "e4m3").T @ v + w2.T @ xs
    f = np.tanh(a + f64(b1)[:, None])
    h = f * f64(gain)[:, None]
    y = (mxq(f64(w3), 0, "e4m3").T @ mxq(h, 0, "e4m3")) + f
    e = (mxq(f64(w4), 0, "e4m3").T @ xs) + f64(b2)[:, None]
    return y * e

@@ -1,0 +1,276 @@
+from contextlib import ExitStack
+
+import concourse.mybir as mybir
+
+K, K2, H, T, S = 1536, 512, 1024, 2048, 512
+FLOPS = 2 * S * H * (K + K2 + H + K2)
+
+F32 = mybir.dt.float32
+BF16 = mybir.dt.bfloat16
+I32 = mybir.dt.int32
+U32 = mybir.dt.uint32
+U16 = mybir.dt.uint16
+U8 = mybir.dt.uint8
+FP8X4 = mybir.dt.float8_e4m3fn_x4
+FP4X4 = mybir.dt.float4_e2m1fn_x4
+ADD = mybir.AluOpType.add
+MULT = mybir.AluOpType.mult
+COPY = mybir.ActivationFunctionType.Copy
+TANH = mybir.ActivationFunctionType.Tanh
+
+P = 128
+PACK = 4
+SPAN = P * PACK
+QUADS = 4
+HALVES = H // SPAN
+PASSES = K // SPAN
+
+
+def tile_list_drilling_steering_features_kernel(
+    tc, tab_words, tab_scales, offs, xs_words, xs_scales, w1, w2_words, w2_scales, b1, gain, w3, w4, b2, out
+):
+    nc = tc.nc
+    with ExitStack() as ctx:
+        keep = ctx.enter_context(tc.tile_pool(name="keep", bufs=1))
+        ring = ctx.enter_context(tc.tile_pool(name="ring", bufs=3))
+        psum = ctx.enter_context(tc.psum_pool(name="psum", bufs=1))
+
+        offsets = keep.tile([P, S // 16], U16, name="offsets")
+        tab_plane = keep.tile([P, T], U8, name="tab_plane", align_bytes=64)
+        w2_plane_raw = keep.tile([P, H], U8, name="w2_plane_raw", align_bytes=64)
+        xs_plane = keep.tile([P, S], U8, name="xs_plane", align_bytes=64)
+        for plane in (tab_plane, w2_plane_raw, xs_plane):
+            nc.vector.memset(plane[:].bitcast(I32), 0)
+
+
+        def load_weight(name, w, a, b):
+            raw = keep.tile([P, PACK, SPAN], F32, name=name)
+            rows = w[a * SPAN : (a + 1) * SPAN, b * SPAN : (b + 1) * SPAN]
+            nc.sync.dma_start(out=raw[:], in_=rows.rearrange("(p j) c -> p j c", j=PACK))
+            return raw
+
+        def load_table(a):
+            words = keep.tile([P, T], I32, name="tab%d" % a, align_bytes=64)
+            nc.sync.dma_start(out=words[:], in_=tab_words[a].rearrange("p n i -> p (n i)").bitcast(I32))
+            return words
+
+        def load_vector(name, vec):
+            cols = keep.tile([P, HALVES, PACK], F32, name=name)
+            nc.sync.dma_start(out=cols[:], in_=vec.rearrange("(b p t) -> p b t", b=HALVES, t=PACK))
+            return cols
+
+        raw = {}
+        tab = {}
+        raw["w1", 0, 0] = load_weight("w1_00", w1, 0, 0)
+        nc.sync.dma_start(offsets[:], offs)
+        tab[0] = load_table(0)
+        xs_codes = keep.tile([P, S], I32, name="xs_codes", align_bytes=64)
+        nc.sync.dma_start(out=xs_codes[:], in_=xs_words[0].rearrange("p n i -> p (n i)").bitcast(I32))
+        w2_raw = keep.tile([P, 2 * H], U8, name="w2_raw", align_bytes=64)
+        nc.sync.dma_start(out=w2_raw[:].bitcast(I32), in_=w2_words[0].bitcast(I32))
+        for q in range(QUADS):
+            nc.sync.dma_start(
+                out=tab_plane[32 * q : 32 * q + 4 * PASSES, :].bitcast(I32),
+                in_=tab_scales[:, 4 * q : 4 * q + 4, :].bitcast(I32),
+            )
+        raw["w1", 1, 0] = load_weight("w1_10", w1, 1, 0)
+        tab[1] = load_table(1)
+        for q in range(QUADS):
+            nc.sync.dma_start(
+                out=w2_plane_raw[32 * q : 32 * q + 4, :].bitcast(I32),
+                in_=w2_scales[0, 4 * q : 4 * q + 4, :].bitcast(I32),
+            )
+        raw["w1", 2, 0] = load_weight("w1_20", w1, 2, 0)
+        tab[2] = load_table(2)
+        b1_cols = load_vector("b1_cols", b1)
+        for q in range(QUADS):
+            nc.sync.dma_start(
+                out=xs_plane[32 * q : 32 * q + 4, :].bitcast(I32),
+                in_=xs_scales[0, 4 * q : 4 * q + 4, :].bitcast(I32),
+            )
+        raw["w1", 0, 1] = load_weight("w1_01", w1, 0, 1)
+        gain_cols = load_vector("gain_cols", gain)
+        raw["w1", 1, 1] = load_weight("w1_11", w1, 1, 1)
+        raw["w1", 2, 1] = load_weight("w1_21", w1, 2, 1)
+        b2_cols = load_vector("b2_cols", b2)
+        raw["w3", 0, 0] = load_weight("w3_00", w3, 0, 0)
+        raw["w3", 1, 0] = load_weight("w3_10", w3, 1, 0)
+        raw["w4", 0, 0] = load_weight("w4_00", w4, 0, 0)
+        raw["w3", 0, 1] = load_weight("w3_01", w3, 0, 1)
+        raw["w3", 1, 1] = load_weight("w3_11", w3, 1, 1)
+        raw["w4", 0, 1] = load_weight("w4_01", w4, 0, 1)
+
+        grouped = {}
+        quantised = {}
+
+        def cast(key, on_vector):
+            grouped[key] = ring.tile([P, SPAN * PACK], BF16, name="grouped", align_bytes=64, bufs=4)
+            dst = grouped[key][:].rearrange("p (t m j) -> p m j t", t=PACK, j=PACK)
+            src = raw[key][:].rearrange("p j (m t) -> p m j t", t=PACK)
+            cut = P - on_vector
+            if cut > 0:
+                nc.scalar.activation(dst[:, :cut], src[:, :cut], COPY)
+            if cut < P:
+                nc.vector.tensor_copy(out=dst[:, cut:], in_=src[:, cut:])
+
+        def quantize(key, pieces=1):
+            name = "%s_%d%d" % key
+            codes = keep.tile([P, SPAN], U32, name=name + "_codes", align_bytes=64)
+            plane = keep.tile([P, SPAN], U8, name=name + "_plane", align_bytes=64)
+            width = SPAN // pieces
+            for c in range(0, SPAN, width):
+                nc.vector.quantize_mx(
+                    out=codes[:, c : c + width].bitcast(FP8X4),
+                    scales=plane[:, c : c + width],
+                    in_=grouped[key][:, PACK * c : PACK * (c + width)],
+                )
+            quantised[key] = (codes, plane)
+
+        def gather(a):
+            words = keep.tile([P, S], U32, name="picked%d" % a, align_bytes=64)
+            nc.vector.tensor_copy(words[:], tab[a][:].bitcast(U32).indirect(offsets[:]))
+            picked[a] = words
+
+        def banks(first):
+            return [psum.tile([P, S], F32, name="bank", tag="bank%d" % (first + t)) for t in range(PACK)]
+
+        def multiply(acc, key, rhs, rhs_scale, start, stop):
+            codes, plane = quantised[key]
+            for t in range(PACK):
+                cols = slice(t * P, (t + 1) * P)
+                nc.tensor.matmul_mx(
+                    out=acc[t][:], lhsT=codes[:, cols].bitcast(FP8X4), lhsT_scale=plane[:, cols],
+                    rhs=rhs, rhs_scale=rhs_scale, start=start, stop=stop,
+                )
+
+        def multiply_w1(a, b, start, stop):
+            multiply(acc1[b], ("w1", a, b), picked[a][:].bitcast(FP8X4), picked_plane[4 * a :, :], start, stop)
+
+        def multiply_w2(b, start):
+            for t in range(PACK):
+                c = b * SPAN + t * P
+                nc.tensor.matmul_mx(
+                    out=acc1[b][t][:], lhsT=w2_codes[:, 2 * c : 2 * (c + P)].bitcast(FP4X4),
+                    lhsT_scale=w2_plane[:, c : c + P],
+                    rhs=xs_codes[:].bitcast(FP8X4), rhs_scale=xs_plane[:], start=start, stop=False,
+                )
+
+        def multiply_w3(acc, a, b):
+            codes, plane = quantised["h", a, 0]
+            multiply(acc, ("w3", a, b), codes[:].bitcast(FP8X4), plane[:], a == 0, a == HALVES - 1)
+
+        def multiply_w4(acc, b):
+            multiply(acc, ("w4", 0, b), xs_codes[:].bitcast(FP8X4), xs_plane[:], True, True)
+
+        def tanh(b):
+            f[b] = keep.tile([P, PACK, S], F32, name="f%d" % b)
+            h_rows[b] = ring.tile([P, PACK, S], BF16, name="h_rows", bufs=1)
+            for t in range(PACK):
+                nc.scalar.activation(f[b][:, t, :], acc1[b][t][:], TANH, bias=b1_cols[:, b, t : t + 1])
+
+        def scale(b, ts):
+            for t in ts:
+                nc.vector.tensor_scalar(h_rows[b][:, t, :], f[b][:, t, :], gain_cols[:, b, t : t + 1], None, MULT)
+
+        def weave(b):
+            grouped["h", b, 0] = ring.tile([P, S * PACK], BF16, name="grouped", align_bytes=64, bufs=4)
+            nc.vector.tensor_copy(
+                out=grouped["h", b, 0][:].rearrange("p (c i t) -> p c t i", t=PACK, i=4),
+                in_=h_rows[b][:].rearrange("p t (c i) -> p c t i", i=4),
+            )
+
+        def residual(acc, b, ts):
+            for t in ts:
+                nc.vector.tensor_tensor(f[b][:, t, :], acc[t][:], f[b][:, t, :], ADD)
+
+        def finish(acc, b, ts):
+            rows = out[b * SPAN : (b + 1) * SPAN, :].rearrange("(p t) j -> p t j", t=PACK)
+            for t in ts:
+                nc.vector.scalar_tensor_tensor(
+                    f[b][:, t, :], acc[t][:], b2_cols[:, b, t : t + 1], f[b][:, t, :], ADD, MULT
+                )
+                nc.sync.dma_start(out=rows[:, t, :], in_=f[b][:, t, :])
+
+        picked_plane = keep.tile([P, S], U8, name="picked_plane", align_bytes=64)
+        w2_codes = keep.tile([P, 2 * H], U8, name="w2_codes", align_bytes=64)
+        w2_plane = keep.tile([P, H], U8, name="w2_plane", align_bytes=64)
+        picked = {}
+        f = {}
+        h_rows = {}
+        acc1 = [banks(0), banks(PACK)]
+
+        def deal_w2():
+            nc.vector.tensor_copy(
+                out=w2_codes[:].rearrange("p (b t m e) -> p b t m e", b=HALVES, t=PACK, e=2),
+                in_=w2_raw[:].rearrange("p (b m t e) -> p b t m e", b=HALVES, t=PACK, e=2),
+            )
+            nc.vector.tensor_copy(
+                out=w2_plane[:].rearrange("p (b t m) -> p b t m", b=HALVES, t=PACK),
+                in_=w2_plane_raw[:].rearrange("p (b m t) -> p b t m", b=HALVES, t=PACK),
+            )
+
+        cast(("w1", 0, 0), 0)
+        nc.vector.tensor_copy(picked_plane[:], tab_plane[:].indirect(offsets[:]))
+        quantize(("w1", 0, 0))
+        gather(0)
+        multiply_w1(0, 0, True, False)
+        deal_w2()
+        cast(("w1", 1, 0), 0)
+        quantize(("w1", 1, 0))
+        gather(1)
+        multiply_w1(1, 0, False, False)
+        cast(("w1", 2, 0), 64)
+        quantize(("w1", 2, 0))
+        multiply_w2(0, False)
+        gather(2)
+        multiply_w1(2, 0, False, True)
+        multiply_w2(1, True)
+        tanh(0)
+        cast(("w1", 0, 1), 128)
+        scale(0, [0, 1])
+        quantize(("w1", 0, 1))
+        multiply_w1(0, 1, False, False)
+        scale(0, [2, 3])
+        cast(("w1", 1, 1), 0)
+        weave(0)
+        quantize(("w1", 1, 1))
+        multiply_w1(1, 1, False, False)
+        cast(("w1", 2, 1), 64)
+        quantize(("w1", 2, 1), 4)
+        multiply_w1(2, 1, False, True)
+        quantize(("h", 0, 0))
+        cast(("w3", 0, 0), 64)
+        tanh(1)
+        scale(1, [0, 1])
+        quantize(("w3", 0, 0))
+        acc2 = banks(0)
+        multiply_w3(acc2, 0, 0)
+        scale(1, [2, 3])
+        cast(("w3", 1, 0), 0)
+        weave(1)
+        quantize(("h", 1, 0))
+        quantize(("w3", 1, 0))
+        multiply_w3(acc2, 1, 0)
+        cast(("w4", 0, 0), 0)
+        residual(acc2, 0, [0, 1])
+        quantize(("w4", 0, 0))
+        acc3 = banks(PACK)
+        multiply_w4(acc3, 0)
+        residual(acc2, 0, [2, 3])
+        cast(("w3", 0, 1), 0)
+        finish(acc3, 0, [0, 1])
+        quantize(("w3", 0, 1))
+        acc2 = banks(0)
+        multiply_w3(acc2, 0, 1)
+        cast(("w3", 1, 1), 0)
+        finish(acc3, 0, [2])
+        quantize(("w3", 1, 1))
+        multiply_w3(acc2, 1, 1)
+        finish(acc3, 0, [3])
+        cast(("w4", 0, 1), 0)
+        residual(acc2, 1, [0, 1])
+        quantize(("w4", 0, 1))
+        acc3 = banks(PACK)
+        multiply_w4(acc3, 1)
+        residual(acc2, 1, [2, 3])
+        finish(acc3, 1, [0, 1, 2, 3])

@@ -16,6 +16,7 @@ FP4X4 = mybir.dt.float4_e2m1fn_x4
 ADD = mybir.AluOpType.add
 MULT = mybir.AluOpType.mult
 COPY = mybir.ActivationFunctionType.Copy
+IDENTITY = mybir.ActivationFunctionType.Identity
 TANH = mybir.ActivationFunctionType.Tanh
 
 P = 128
@@ -103,15 +104,43 @@ def tile_list_drilling_steering_features_kernel(
         grouped = {}
         quantised = {}
 
-        def cast(key, on_vector):
-            grouped[key] = ring.tile([P, SPAN * PACK], BF16, name="grouped", align_bytes=64, bufs=4)
+        def on_scalar(dst, src):
+            nc.scalar.activation(dst, src, COPY)
+
+        def on_vector(dst, src):
+            nc.vector.tensor_copy(out=dst, in_=src)
+
+        def round_on(engine, key, lo, hi):
+            if key not in grouped:
+                grouped[key] = ring.tile([P, SPAN * PACK], BF16, name="grouped", align_bytes=64, bufs=6)
             dst = grouped[key][:].rearrange("p (t m j) -> p m j t", t=PACK, j=PACK)
             src = raw[key][:].rearrange("p j (m t) -> p m j t", t=PACK)
-            cut = P - on_vector
-            if cut > 0:
-                nc.scalar.activation(dst[:, :cut], src[:, :cut], COPY)
-            if cut < P:
-                nc.vector.tensor_copy(out=dst[:, cut:], in_=src[:, cut:])
+            engine(dst[:, lo:hi], src[:, lo:hi])
+
+        def tanh_part(b, lo, hi):
+            if b not in f:
+                f[b] = keep.tile([P, PACK, S], F32, name="f%d" % b)
+            for t in range(PACK):
+                nc.scalar.activation(f[b][:, t, lo:hi], acc1[b][t][:, lo:hi], TANH, bias=b1_cols[:, b, t : t + 1])
+
+        def weigh(b, lo, hi):
+            key = ("h", b, 0)
+            if key not in grouped:
+                grouped[key] = ring.tile([P, SPAN * PACK], BF16, name="grouped", align_bytes=64, bufs=6)
+            nc.vector.tensor_tensor(
+                grouped[key][:, PACK * lo : PACK * hi].rearrange("p (c i t) -> p c t i", t=PACK, i=2),
+                f[b][:, :, lo:hi].rearrange("p t (c i) -> p c t i", i=2),
+                gain_cols[:, b, :].unsqueeze(1).unsqueeze(3).to_broadcast([P, (hi - lo) // 2, PACK, 2]),
+                MULT,
+            )
+
+        def finish_aside(acc, b, ts):
+            rows = out[b * SPAN : (b + 1) * SPAN, :].rearrange("(p t) j -> p t j", t=PACK)
+            for t in ts:
+                e = ring.tile([P, S], F32, name="e", bufs=2)
+                nc.scalar.activation(e[:], acc[t][:], IDENTITY, bias=b2_cols[:, b, t : t + 1])
+                nc.gpsimd.tensor_tensor(f[b][:, t, :], f[b][:, t, :], e[:], MULT)
+                nc.sync.dma_start(out=rows[:, t, :], in_=f[b][:, t, :])
 
         def quantize(key, pieces=1):
             name = "%s_%d%d" % key
@@ -173,7 +202,7 @@ def tile_list_drilling_steering_features_kernel(
                 nc.vector.tensor_scalar(h_rows[b][:, t, :], f[b][:, t, :], gain_cols[:, b, t : t + 1], None, MULT)
 
         def weave(b):
-            grouped["h", b, 0] = ring.tile([P, S * PACK], BF16, name="grouped", align_bytes=64, bufs=4)
+            grouped["h", b, 0] = ring.tile([P, S * PACK], BF16, name="grouped", align_bytes=64, bufs=6)
             nc.vector.tensor_copy(
                 out=grouped["h", b, 0][:].rearrange("p (c i t) -> p c t i", t=PACK, i=4),
                 in_=h_rows[b][:].rearrange("p t (c i) -> p c t i", i=4),
@@ -209,65 +238,69 @@ def tile_list_drilling_steering_features_kernel(
                 in_=w2_plane_raw[:].rearrange("p (b m t) -> p b t m", b=HALVES, t=PACK),
             )
 
-        cast(("w1", 0, 0), 0)
+        round_on(on_scalar, ("w1", 0, 0), 0, 128)
         nc.vector.tensor_copy(picked_plane[:], tab_plane[:].indirect(offsets[:]))
         quantize(("w1", 0, 0))
         gather(0)
         multiply_w1(0, 0, True, False)
         deal_w2()
-        cast(("w1", 1, 0), 0)
+        round_on(on_scalar, ("w1", 1, 0), 0, 128)
         quantize(("w1", 1, 0))
         gather(1)
         multiply_w1(1, 0, False, False)
-        cast(("w1", 2, 0), 64)
+        round_on(on_scalar, ("w1", 2, 0), 0, 64)
+        round_on(on_vector, ("w1", 2, 0), 64, 128)
         quantize(("w1", 2, 0))
         multiply_w2(0, False)
         gather(2)
         multiply_w1(2, 0, False, True)
         multiply_w2(1, True)
-        tanh(0)
-        cast(("w1", 0, 1), 128)
-        scale(0, [0, 1])
+        tanh_part(0, 0, 512)
+        round_on(on_vector, ("w1", 0, 1), 0, 128)
         quantize(("w1", 0, 1))
         multiply_w1(0, 1, False, False)
-        scale(0, [2, 3])
-        cast(("w1", 1, 1), 0)
-        weave(0)
+        round_on(on_scalar, ("w1", 1, 1), 0, 64)
+        round_on(on_vector, ("w1", 1, 1), 64, 128)
+        weigh(0, 0, 256)
         quantize(("w1", 1, 1))
         multiply_w1(1, 1, False, False)
-        cast(("w1", 2, 1), 64)
+        round_on(on_scalar, ("w1", 2, 1), 0, 96)
+        round_on(on_vector, ("w1", 2, 1), 96, 128)
+        weigh(0, 256, 512)
         quantize(("w1", 2, 1), 4)
         multiply_w1(2, 1, False, True)
+        round_on(on_scalar, ("w3", 0, 0), 0, 64)
         quantize(("h", 0, 0))
-        cast(("w3", 0, 0), 64)
-        tanh(1)
-        scale(1, [0, 1])
+        round_on(on_vector, ("w3", 0, 0), 64, 128)
+        tanh_part(1, 0, 256)
         quantize(("w3", 0, 0))
         acc2 = banks(0)
         multiply_w3(acc2, 0, 0)
-        scale(1, [2, 3])
-        cast(("w3", 1, 0), 0)
-        weave(1)
+        weigh(1, 0, 256)
+        tanh_part(1, 256, 512)
+        round_on(on_scalar, ("w3", 1, 0), 0, 96)
+        round_on(on_vector, ("w3", 1, 0), 96, 128)
+        weigh(1, 256, 512)
         quantize(("h", 1, 0))
-        quantize(("w3", 1, 0))
+        quantize(("w3", 1, 0), 4)
         multiply_w3(acc2, 1, 0)
-        cast(("w4", 0, 0), 0)
-        residual(acc2, 0, [0, 1])
+        round_on(on_scalar, ("w4", 0, 0), 0, 96)
+        round_on(on_vector, ("w4", 0, 0), 96, 128)
+        residual(acc2, 0, [0])
         quantize(("w4", 0, 0))
         acc3 = banks(PACK)
         multiply_w4(acc3, 0)
-        residual(acc2, 0, [2, 3])
-        cast(("w3", 0, 1), 0)
-        finish(acc3, 0, [0, 1])
+        residual(acc2, 0, [1, 2, 3])
+        round_on(on_scalar, ("w3", 0, 1), 0, 128)
         quantize(("w3", 0, 1))
         acc2 = banks(0)
         multiply_w3(acc2, 0, 1)
-        cast(("w3", 1, 1), 0)
-        finish(acc3, 0, [2])
+        finish(acc3, 0, [0, 1])
+        round_on(on_scalar, ("w3", 1, 1), 0, 128)
         quantize(("w3", 1, 1))
         multiply_w3(acc2, 1, 1)
-        finish(acc3, 0, [3])
-        cast(("w4", 0, 1), 0)
+        finish(acc3, 0, [2, 3])
+        round_on(on_scalar, ("w4", 0, 1), 0, 128)
         residual(acc2, 1, [0, 1])
         quantize(("w4", 0, 1))
         acc3 = banks(PACK)

from contextlib import ExitStack

import concourse.mybir as mybir

K, K2, H, T, S = 1536, 512, 1024, 2048, 512
FLOPS = 2 * S * H * (K + K2 + H + K2)

F32 = mybir.dt.float32
BF16 = mybir.dt.bfloat16
I32 = mybir.dt.int32
U32 = mybir.dt.uint32
U16 = mybir.dt.uint16
U8 = mybir.dt.uint8
FP8X4 = mybir.dt.float8_e4m3fn_x4
FP4X4 = mybir.dt.float4_e2m1fn_x4
ADD = mybir.AluOpType.add
MULT = mybir.AluOpType.mult
COPY = mybir.ActivationFunctionType.Copy
IDENTITY = mybir.ActivationFunctionType.Identity
TANH = mybir.ActivationFunctionType.Tanh

P = 128
PACK = 4
SPAN = P * PACK
QUADS = 4
HALVES = H // SPAN
PASSES = K // SPAN


def tile_list_drilling_steering_features_kernel(
    tc, tab_words, tab_scales, offs, xs_words, xs_scales, w1, w2_words, w2_scales, b1, gain, w3, w4, b2, out
):
    nc = tc.nc
    with ExitStack() as ctx:
        keep = ctx.enter_context(tc.tile_pool(name="keep", bufs=1))
        ring = ctx.enter_context(tc.tile_pool(name="ring", bufs=3))
        psum = ctx.enter_context(tc.psum_pool(name="psum", bufs=1))

        offsets = keep.tile([P, S // 16], U16, name="offsets")
        tab_plane = keep.tile([P, T], U8, name="tab_plane", align_bytes=64)
        w2_plane_raw = keep.tile([P, H], U8, name="w2_plane_raw", align_bytes=64)
        xs_plane = keep.tile([P, S], U8, name="xs_plane", align_bytes=64)
        for plane in (tab_plane, w2_plane_raw, xs_plane):
            nc.vector.memset(plane[:].bitcast(I32), 0)


        def load_weight(name, w, a, b):
            raw = keep.tile([P, PACK, SPAN], F32, name=name)
            rows = w[a * SPAN : (a + 1) * SPAN, b * SPAN : (b + 1) * SPAN]
            nc.sync.dma_start(out=raw[:], in_=rows.rearrange("(p j) c -> p j c", j=PACK))
            return raw

        def load_table(a):
            words = keep.tile([P, T], I32, name="tab%d" % a, align_bytes=64)
            nc.sync.dma_start(out=words[:], in_=tab_words[a].rearrange("p n i -> p (n i)").bitcast(I32))
            return words

        def load_vector(name, vec):
            cols = keep.tile([P, HALVES, PACK], F32, name=name)
            nc.sync.dma_start(out=cols[:], in_=vec.rearrange("(b p t) -> p b t", b=HALVES, t=PACK))
            return cols

        raw = {}
        tab = {}
        raw["w1", 0, 0] = load_weight("w1_00", w1, 0, 0)
        nc.sync.dma_start(offsets[:], offs)
        tab[0] = load_table(0)
        xs_codes = keep.tile([P, S], I32, name="xs_codes", align_bytes=64)
        nc.sync.dma_start(out=xs_codes[:], in_=xs_words[0].rearrange("p n i -> p (n i)").bitcast(I32))
        w2_raw = keep.tile([P, 2 * H], U8, name="w2_raw", align_bytes=64)
        nc.sync.dma_start(out=w2_raw[:].bitcast(I32), in_=w2_words[0].bitcast(I32))
        for q in range(QUADS):
            nc.sync.dma_start(
                out=tab_plane[32 * q : 32 * q + 4 * PASSES, :].bitcast(I32),
                in_=tab_scales[:, 4 * q : 4 * q + 4, :].bitcast(I32),
            )
        raw["w1", 1, 0] = load_weight("w1_10", w1, 1, 0)
        tab[1] = load_table(1)
        for q in range(QUADS):
            nc.sync.dma_start(
                out=w2_plane_raw[32 * q : 32 * q + 4, :].bitcast(I32),
                in_=w2_scales[0, 4 * q : 4 * q + 4, :].bitcast(I32),
            )
        raw["w1", 2, 0] = load_weight("w1_20", w1, 2, 0)
        tab[2] = load_table(2)
        b1_cols = load_vector("b1_cols", b1)
        for q in range(QUADS):
            nc.sync.dma_start(
                out=xs_plane[32 * q : 32 * q + 4, :].bitcast(I32),
                in_=xs_scales[0, 4 * q : 4 * q + 4, :].bitcast(I32),
            )
        raw["w1", 0, 1] = load_weight("w1_01", w1, 0, 1)
        gain_cols = load_vector("gain_cols", gain)
        raw["w1", 1, 1] = load_weight("w1_11", w1, 1, 1)
        raw["w1", 2, 1] = load_weight("w1_21", w1, 2, 1)
        b2_cols = load_vector("b2_cols", b2)
        raw["w3", 0, 0] = load_weight("w3_00", w3, 0, 0)
        raw["w3", 1, 0] = load_weight("w3_10", w3, 1, 0)
        raw["w4", 0, 0] = load_weight("w4_00", w4, 0, 0)
        raw["w3", 0, 1] = load_weight("w3_01", w3, 0, 1)
        raw["w3", 1, 1] = load_weight("w3_11", w3, 1, 1)
        raw["w4", 0, 1] = load_weight("w4_01", w4, 0, 1)

        grouped = {}
        quantised = {}

        def on_scalar(dst, src):
            nc.scalar.activation(dst, src, COPY)

        def on_vector(dst, src):
            nc.vector.tensor_copy(out=dst, in_=src)

        def round_on(engine, key, lo, hi):
            if key not in grouped:
                grouped[key] = ring.tile([P, SPAN * PACK], BF16, name="grouped", align_bytes=64, bufs=6)
            dst = grouped[key][:].rearrange("p (t m j) -> p m j t", t=PACK, j=PACK)
            src = raw[key][:].rearrange("p j (m t) -> p m j t", t=PACK)
            engine(dst[:, lo:hi], src[:, lo:hi])

        def tanh_part(b, lo, hi):
            if b not in f:
                f[b] = keep.tile([P, PACK, S], F32, name="f%d" % b)
            for t in range(PACK):
                nc.scalar.activation(f[b][:, t, lo:hi], acc1[b][t][:, lo:hi], TANH, bias=b1_cols[:, b, t : t + 1])

        def weigh(b, lo, hi):
            key = ("h", b, 0)
            if key not in grouped:
                grouped[key] = ring.tile([P, SPAN * PACK], BF16, name="grouped", align_bytes=64, bufs=6)
            nc.vector.tensor_tensor(
                grouped[key][:, PACK * lo : PACK * hi].rearrange("p (c i t) -> p c t i", t=PACK, i=2),
                f[b][:, :, lo:hi].rearrange("p t (c i) -> p c t i", i=2),
                gain_cols[:, b, :].unsqueeze(1).unsqueeze(3).to_broadcast([P, (hi - lo) // 2, PACK, 2]),
                MULT,
            )

        def finish_aside(acc, b, ts):
            rows = out[b * SPAN : (b + 1) * SPAN, :].rearrange("(p t) j -> p t j", t=PACK)
            for t in ts:
                e = ring.tile([P, S], F32, name="e", bufs=2)
                nc.scalar.activation(e[:], acc[t][:], IDENTITY, bias=b2_cols[:, b, t : t + 1])
                nc.gpsimd.tensor_tensor(f[b][:, t, :], f[b][:, t, :], e[:], MULT)
                nc.sync.dma_start(out=rows[:, t, :], in_=f[b][:, t, :])

        def quantize(key, pieces=1):
            name = "%s_%d%d" % key
            codes = keep.tile([P, SPAN], U32, name=name + "_codes", align_bytes=64)
            plane = keep.tile([P, SPAN], U8, name=name + "_plane", align_bytes=64)
            width = SPAN // pieces
            for c in range(0, SPAN, width):
                nc.vector.quantize_mx(
                    out=codes[:, c : c + width].bitcast(FP8X4),
                    scales=plane[:, c : c + width],
                    in_=grouped[key][:, PACK * c : PACK * (c + width)],
                )
            quantised[key] = (codes, plane)

        def gather(a):
            words = keep.tile([P, S], U32, name="picked%d" % a, align_bytes=64)
            nc.vector.tensor_copy(words[:], tab[a][:].bitcast(U32).indirect(offsets[:]))
            picked[a] = words

        def banks(first):
            return [psum.tile([P, S], F32, name="bank", tag="bank%d" % (first + t)) for t in range(PACK)]

        def multiply(acc, key, rhs, rhs_scale, start, stop):
            codes, plane = quantised[key]
            for t in range(PACK):
                cols = slice(t * P, (t + 1) * P)
                nc.tensor.matmul_mx(
                    out=acc[t][:], lhsT=codes[:, cols].bitcast(FP8X4), lhsT_scale=plane[:, cols],
                    rhs=rhs, rhs_scale=rhs_scale, start=start, stop=stop,
                )

        def multiply_w1(a, b, start, stop):
            multiply(acc1[b], ("w1", a, b), picked[a][:].bitcast(FP8X4), picked_plane[4 * a :, :], start, stop)

        def multiply_w2(b, start):
            for t in range(PACK):
                c = b * SPAN + t * P
                nc.tensor.matmul_mx(
                    out=acc1[b][t][:], lhsT=w2_codes[:, 2 * c : 2 * (c + P)].bitcast(FP4X4),
                    lhsT_scale=w2_plane[:, c : c + P],
                    rhs=xs_codes[:].bitcast(FP8X4), rhs_scale=xs_plane[:], start=start, stop=False,
                )

        def multiply_w3(acc, a, b):
            codes, plane = quantised["h", a, 0]
            multiply(acc, ("w3", a, b), codes[:].bitcast(FP8X4), plane[:], a == 0, a == HALVES - 1)

        def multiply_w4(acc, b):
            multiply(acc, ("w4", 0, b), xs_codes[:].bitcast(FP8X4), xs_plane[:], True, True)

        def tanh(b):
            f[b] = keep.tile([P, PACK, S], F32, name="f%d" % b)
            h_rows[b] = ring.tile([P, PACK, S], BF16, name="h_rows", bufs=1)
            for t in range(PACK):
                nc.scalar.activation(f[b][:, t, :], acc1[b][t][:], TANH, bias=b1_cols[:, b, t : t + 1])

        def scale(b, ts):
            for t in ts:
                nc.vector.tensor_scalar(h_rows[b][:, t, :], f[b][:, t, :], gain_cols[:, b, t : t + 1], None, MULT)

        def weave(b):
            grouped["h", b, 0] = ring.tile([P, S * PACK], BF16, name="grouped", align_bytes=64, bufs=6)
            nc.vector.tensor_copy(
                out=grouped["h", b, 0][:].rearrange("p (c i t) -> p c t i", t=PACK, i=4),
                in_=h_rows[b][:].rearrange("p t (c i) -> p c t i", i=4),
            )

        def residual(acc, b, ts):
            for t in ts:
                nc.vector.tensor_tensor(f[b][:, t, :], acc[t][:], f[b][:, t, :], ADD)

        def finish(acc, b, ts):
            rows = out[b * SPAN : (b + 1) * SPAN, :].rearrange("(p t) j -> p t j", t=PACK)
            for t in ts:
                nc.vector.scalar_tensor_tensor(
                    f[b][:, t, :], acc[t][:], b2_cols[:, b, t : t + 1], f[b][:, t, :], ADD, MULT
                )
                nc.sync.dma_start(out=rows[:, t, :], in_=f[b][:, t, :])

        picked_plane = keep.tile([P, S], U8, name="picked_plane", align_bytes=64)
        w2_codes = keep.tile([P, 2 * H], U8, name="w2_codes", align_bytes=64)
        w2_plane = keep.tile([P, H], U8, name="w2_plane", align_bytes=64)
        picked = {}
        f = {}
        h_rows = {}
        acc1 = [banks(0), banks(PACK)]

        def deal_w2():
            nc.vector.tensor_copy(
                out=w2_codes[:].rearrange("p (b t m e) -> p b t m e", b=HALVES, t=PACK, e=2),
                in_=w2_raw[:].rearrange("p (b m t e) -> p b t m e", b=HALVES, t=PACK, e=2),
            )
            nc.vector.tensor_copy(
                out=w2_plane[:].rearrange("p (b t m) -> p b t m", b=HALVES, t=PACK),
                in_=w2_plane_raw[:].rearrange("p (b m t) -> p b t m", b=HALVES, t=PACK),
            )

        round_on(on_scalar, ("w1", 0, 0), 0, 128)
        nc.vector.tensor_copy(picked_plane[:], tab_plane[:].indirect(offsets[:]))
        quantize(("w1", 0, 0))
        gather(0)
        multiply_w1(0, 0, True, False)
        deal_w2()
        round_on(on_scalar, ("w1", 1, 0), 0, 128)
        quantize(("w1", 1, 0))
        gather(1)
        multiply_w1(1, 0, False, False)
        round_on(on_scalar, ("w1", 2, 0), 0, 64)
        round_on(on_vector, ("w1", 2, 0), 64, 128)
        quantize(("w1", 2, 0))
        multiply_w2(0, False)
        gather(2)
        multiply_w1(2, 0, False, True)
        multiply_w2(1, True)
        tanh_part(0, 0, 512)
        round_on(on_vector, ("w1", 0, 1), 0, 128)
        quantize(("w1", 0, 1))
        multiply_w1(0, 1, False, False)
        round_on(on_scalar, ("w1", 1, 1), 0, 64)
        round_on(on_vector, ("w1", 1, 1), 64, 128)
        weigh(0, 0, 256)
        quantize(("w1", 1, 1))
        multiply_w1(1, 1, False, False)
        round_on(on_scalar, ("w1", 2, 1), 0, 96)
        round_on(on_vector, ("w1", 2, 1), 96, 128)
        weigh(0, 256, 512)
        quantize(("w1", 2, 1), 4)
        multiply_w1(2, 1, False, True)
        round_on(on_scalar, ("w3", 0, 0), 0, 64)
        quantize(("h", 0, 0))
        round_on(on_vector, ("w3", 0, 0), 64, 128)
        tanh_part(1, 0, 256)
        quantize(("w3", 0, 0))
        acc2 = banks(0)
        multiply_w3(acc2, 0, 0)
        weigh(1, 0, 256)
        tanh_part(1, 256, 512)
        round_on(on_scalar, ("w3", 1, 0), 0, 96)
        round_on(on_vector, ("w3", 1, 0), 96, 128)
        weigh(1, 256, 512)
        quantize(("h", 1, 0))
        quantize(("w3", 1, 0), 4)
        multiply_w3(acc2, 1, 0)
        round_on(on_scalar, ("w4", 0, 0), 0, 96)
        round_on(on_vector, ("w4", 0, 0), 96, 128)
        residual(acc2, 0, [0])
        quantize(("w4", 0, 0))
        acc3 = banks(PACK)
        multiply_w4(acc3, 0)
        residual(acc2, 0, [1, 2, 3])
        round_on(on_scalar, ("w3", 0, 1), 0, 128)
        quantize(("w3", 0, 1))
        acc2 = banks(0)
        multiply_w3(acc2, 0, 1)
        finish(acc3, 0, [0, 1])
        round_on(on_scalar, ("w3", 1, 1), 0, 128)
        quantize(("w3", 1, 1))
        multiply_w3(acc2, 1, 1)
        finish(acc3, 0, [2, 3])
        round_on(on_scalar, ("w4", 0, 1), 0, 128)
        residual(acc2, 1, [0, 1])
        quantize(("w4", 0, 1))
        acc3 = banks(PACK)
        multiply_w4(acc3, 1)
        residual(acc2, 1, [2, 3])
        finish(acc3, 1, [0, 1, 2, 3])
